import numpy as np
import ml_dtypes


def mxq(x, axis, fmt="e4m3"):
    dtype, down = {"e4m3": (ml_dtypes.float8_e4m3fn, 7), "e5m2": (ml_dtypes.float8_e5m2, 14)}[fmt]
    v = np.moveaxis(np.asarray(x, np.float32).astype(ml_dtypes.bfloat16).astype(np.float64), axis, -1)
    blocks = v.reshape(v.shape[:-1] + (-1, 32))
    amax = np.abs(blocks).max(-1, keepdims=True)
    byte = np.maximum(np.where(amax > 0, np.frexp(amax)[1] - 1 + 127, 0) - down, 1)
    scale = np.exp2(byte - 127.0)
    codes = (blocks / scale).astype(np.float32).astype(dtype).astype(np.float64)
    return np.moveaxis((codes * scale).reshape(v.shape), -1, axis)


WIDE = False


def mx_kscale(k):
    if not WIDE:
        return np.ones(k)
    levels = np.array([10, -10, 5, -5, 0])
    if k % 512:
        return np.exp2(np.random.permutation(np.resize(levels, k // 32))).repeat(32)
    a = np.empty((k // 512, 16))
    for p in range(k // 512):
        a[p, :8] = np.random.permutation(np.resize(levels, 8))
        for g in range(8):
            far = levels[np.abs(levels - a[p, g]) >= 10]
            a[p, g + 8] = far[np.random.randint(len(far))]
    return np.exp2(a.ravel()).repeat(32)


def f64(x):
    return np.asarray(x).astype(np.float64)


def striped8(idx):
    return np.concatenate([v.reshape(-1, 16).T for v in idx]).astype(np.uint16)


def unstriped8(offs):
    return np.stack([offs[16 * g:16 * g + 16].T.reshape(-1) for g in range(8)]).astype(np.int64)


E2M1 = np.array([0.0, 0.5, 1.0, 1.5, 2.0, 3.0, 4.0, 6.0, -0.0, -0.5, -1.0, -1.5, -2.0, -3.0, -4.0, -6.0])


def pack_weight(w, fmt):
    k, n = w.shape
    w = f64(np.asarray(w, np.float32).astype(ml_dtypes.bfloat16)).reshape(k // 32, 32, n)
    amax = np.abs(w).max(1)
    if fmt == "e4m3":
        byte = np.frexp(amax)[1] - 1 + 127 - 7
    else:
        mant, ex = np.frexp(amax / 6.0)
        byte = np.where(mant > 0.5, ex, ex - 1) + 127
    byte = np.clip(np.where(amax > 0, byte, 1), 1, 254)
    scaled = (w * np.exp2(127.0 - byte)[:, None, :]).reshape(k, n).astype(np.float32)
    by_word = np.ascontiguousarray(scaled.reshape(k // 512, 128, 4, n).transpose(0, 1, 3, 2))
    if fmt == "e4m3":
        words = by_word.astype(ml_dtypes.float8_e4m3fn).view(np.uint8)
    else:
        c = by_word.astype(ml_dtypes.float4_e2m1fn).view(np.uint8) & 0xF
        words = (c[..., 0::2] | (c[..., 1::2] << 4)).reshape(k // 512, 128, 2 * n)
    return np.ascontiguousarray(words), np.ascontiguousarray(byte.astype(np.uint8).reshape(k // 512, 16, n))


def unpack_weight(words, scales, fmt):
    g, _, n = scales.shape
    words = np.ascontiguousarray(words).reshape(g, 128, n, -1)
    if fmt == "e4m3":
        vals = words.view(ml_dtypes.float8_e4m3fn).astype(np.float64)
    else:
        nib = np.empty((g, 128, n, 4), np.uint8)
        nib[..., 0::2] = words & 0xF
        nib[..., 1::2] = words >> 4
        vals = E2M1[nib]
    vals = vals * np.repeat(np.exp2(scales.astype(np.float64) - 127.0), 8, axis=1)[..., None]
    return vals.transpose(0, 1, 3, 2).reshape(g * 512, n)


K, M, T, S = 2048, 128, 2048, 1024


def setup_inputs():
    n = np.random.standard_normal
    s = mx_kscale(K)[:, None]
    s2 = mx_kscale(512)[:, None]
    p_w4 = pack_weight(n((K, M)) / np.sqrt(K) / s, "e2m1")
    return {
        "x": (n((K, S)) * s).astype(np.float32),
        "w4_words": p_w4[0],
        "w4_scales": p_w4[1],
        "c": (n((512, S)) * s2).astype(np.float32),
        "u": (n((512, M)) / np.sqrt(512) / s2).astype(np.float32),
        "wgo": np.repeat(np.random.uniform(0.5, 2.0, (8, S)), 16, axis=0).astype(np.float32),
        "offs": striped8(np.stack([np.random.permutation(T)[:S] for _ in range(8)])),
    }


def reference(x, w4_words, w4_scales, c, u, wgo, offs):
    x_ = mxq(f64(x), 0, "e4m3")
    w4_ = unpack_weight(w4_words, w4_scales, "e2m1")
    c_ = mxq(f64(c), 0, "e4m3")
    u_ = mxq(f64(u), 0, "e4m3")
    y = w4_.T @ x_ + u_.T @ c_
    place = unstriped8(offs)[np.arange(M) % 128 // 16]
    out = np.zeros((M, T))
    out[np.arange(M)[:, None], place] = f64(wgo)[np.arange(M) % 128] * (y)
    return out

@@ -1,0 +1,138 @@
+from contextlib import ExitStack
+
+import concourse.mybir as mybir
+
+K, M, T, S, L = 2048, 128, 2048, 1024, 512
+FLOPS = 2 * (K + L) * M * S
+
+F32 = mybir.dt.float32
+BF16 = mybir.dt.bfloat16
+I32 = mybir.dt.int32
+U32 = mybir.dt.uint32
+U16 = mybir.dt.uint16
+U8 = mybir.dt.uint8
+FP8X4 = mybir.dt.float8_e4m3fn_x4
+FP4X4 = mybir.dt.float4_e2m1fn_x4
+
+P = 128
+PACK = 4
+K_PASS = P * PACK
+X_PASSES = K // K_PASS
+HALF = S // 2
+
+LOADS = [(0, 0, 512, 320), (1, 0, 512, 320), (2, 0, 512, 320), (3, 0, 512, 320), (4, 0, 512, 256),
+         (0, 512, 512, 512), (1, 512, 512, 512), (2, 512, 512, 320), (3, 512, 512, 320),
+         (4, 512, 256, 128), (4, 768, 128, 64), (4, 896, 128, 48)]
+GROUPS = [(0, 512, "v"), (512, 128, "s"), (640, 128, "s"), (768, 128, "s"), (896, 128, "s")]
+SCATTERS = [(0, 512), (512, 512)]
+SMALL = [("words", 0), ("s0", 0), ("s1", 1), ("s2", 1), ("s3", 2), ("u", 2), ("offs", 3), ("g0", 4), ("g1", 11)]
+
+
+def tile_list_hscat_d_none_kernel(tc, x, w4_words, w4_scales, c, u, wgo, offs, out):
+    nc = tc.nc
+
+    def interleave(engine_copy, dst, src, lo, hi):
+        engine_copy(
+            out=dst[:, lo:hi, :].rearrange("p (c i) t -> p c t i", i=4),
+            in_=src[:, :, lo:hi].rearrange("p t (c i) -> p c t i", i=4),
+        )
+
+    with ExitStack() as ctx:
+        keep = ctx.enter_context(tc.tile_pool(name="keep", bufs=1))
+        psum = ctx.enter_context(tc.psum_pool(name="psum", bufs=1))
+
+        offsets = keep.tile([P, S // 16], U16, name="offsets")
+        window = keep.tile([P, T], F32, name="window")
+        w_words = keep.tile([P, X_PASSES, 2 * M], U8, name="w_words", align_bytes=64)
+        w_scales = keep.tile([P, X_PASSES, M], U8, name="w_scales", align_bytes=64)
+        u_raw = keep.tile([P, PACK, M], F32, name="u_raw")
+        gains = [keep.tile([P, w], F32, name="gain%d" % i) for i, (s0, w) in enumerate(SCATTERS)]
+        sums = [keep.tile([P, w], F32, name="sum%d" % i) for i, (s0, w) in enumerate(SCATTERS)]
+
+        nc.vector.memset(w_scales[:].rearrange("p a n -> p (a n)").bitcast(I32), 0)
+        nc.vector.memset(window[:], 0.0)
+
+        def small_load(name):
+            if name == "offs":
+                nc.sync.dma_start(offsets[:], offs)
+            elif name == "words":
+                nc.sync.dma_start(out=w_words[:].bitcast(I32), in_=w4_words.rearrange("a p b -> p a b").bitcast(I32))
+            elif name == "u":
+                nc.sync.dma_start(out=u_raw[:], in_=u.rearrange("(p j) n -> p j n", j=PACK))
+            elif name[0] == "s":
+                q = int(name[1])
+                nc.sync.dma_start(
+                    out=w_scales[32 * q : 32 * q + 4, :, :].bitcast(I32),
+                    in_=w4_scales[:, 4 * q : 4 * q + 4, :].rearrange("a r n -> r a n").bitcast(I32),
+                )
+            else:
+                i = int(name[1])
+                s0, w = SCATTERS[i]
+                nc.sync.dma_start(out=gains[i][:], in_=wgo[:, s0 : s0 + w])
+
+        raws = []
+        for i, (a, c0, w, ws) in enumerate(LOADS):
+            rows = x[a * K_PASS : (a + 1) * K_PASS, :] if a < X_PASSES else c
+            raw = keep.tile([P, PACK, w], F32, name="raw%d" % i)
+            nc.sync.dma_start(out=raw[:], in_=rows[:, c0 : c0 + w].rearrange("(p j) w -> p j w", j=PACK))
+            raws.append(raw)
+            for name, at in SMALL:
+                if at == i:
+                    small_load(name)
+
+        u_codes = keep.tile([P, M], U32, name="u_codes", align_bytes=64)
+        u_scales = keep.tile([P, M], U8, name="u_scales", align_bytes=64)
+        banks = [psum.tile([P, w], F32, name="bank%d" % g) for g, (g0, w, e) in enumerate(GROUPS)]
+        done = [0 for g in GROUPS]
+        emptied = [0 for s in SCATTERS]
+
+        for i, (a, c0, w, ws) in enumerate(LOADS):
+            grouped = keep.tile([P, w, PACK], BF16, name="grouped%d" % i, align_bytes=64)
+            codes = keep.tile([P, w], U32, name="codes%d" % i, align_bytes=64)
+            scales = keep.tile([P, w], U8, name="scales%d" % i, align_bytes=64)
+            for h0 in range(0, w, HALF):
+                hw = min(HALF, w)
+                if ws > 0:
+                    interleave(nc.scalar.copy, grouped, raws[i], h0, h0 + ws)
+                if ws < hw:
+                    interleave(nc.vector.tensor_copy, grouped, raws[i], h0 + ws, h0 + hw)
+                nc.vector.quantize_mx(
+                    out=codes[:, h0 : h0 + hw].bitcast(FP8X4),
+                    scales=scales[:, h0 : h0 + hw],
+                    in_=grouped[:, h0 : h0 + hw, :].rearrange("p w j -> p (w j)"),
+                )
+            if i == 3:
+                u_grouped = keep.tile([P, M, PACK], BF16, name="u_grouped", align_bytes=64)
+                interleave(nc.vector.tensor_copy, u_grouped, u_raw, 0, M)
+                nc.vector.quantize_mx(
+                    out=u_codes[:].bitcast(FP8X4), scales=u_scales[:], in_=u_grouped[:].rearrange("p w j -> p (w j)")
+                )
+            for g, (g0, gw, eng) in enumerate(GROUPS):
+                if g0 < c0 or g0 + gw > c0 + w:
+                    continue
+                cols = slice(g0 - c0, g0 - c0 + gw)
+                nc.tensor.matmul_mx(
+                    out=banks[g][:],
+                    lhsT=w_words[:, a, :].bitcast(FP4X4) if a < X_PASSES else u_codes[:].bitcast(FP8X4),
+                    lhsT_scale=w_scales[:, a, :] if a < X_PASSES else u_scales[:],
+                    rhs=codes[:, cols].bitcast(FP8X4),
+                    rhs_scale=scales[:, cols],
+                    start=(done[g] == 0),
+                    stop=(done[g] == X_PASSES),
+                )
+                done[g] += 1
+                if done[g] == X_PASSES + 1:
+                    s = [k for k, (s0, sw) in enumerate(SCATTERS) if s0 <= g0 < s0 + sw][0]
+                    s0, sw = SCATTERS[s]
+                    copy = nc.vector.tensor_copy if eng == "v" else nc.scalar.copy
+                    copy(out=sums[s][:, g0 - s0 : g0 - s0 + gw], in_=banks[g][:])
+                    emptied[s] += gw
+                    if emptied[s] == sw:
+                        nc.vector.tensor_tensor(
+                            window[:].indirect(offsets[:, s0 // 16 : (s0 + sw) // 16]),
+                            sums[s][:],
+                            gains[s][:],
+                            mybir.AluOpType.mult,
+                        )
+
+        nc.sync.dma_start(out=out, in_=window[:])

@@ -20,12 +20,10 @@ K_PASS = P * PACK
 X_PASSES = K // K_PASS
 HALF = S // 2
 
-LOADS = [(0, 0, 512, 320), (1, 0, 512, 320), (2, 0, 512, 320), (3, 0, 512, 320), (4, 0, 512, 256),
-         (0, 512, 512, 512), (1, 512, 512, 512), (2, 512, 512, 320), (3, 512, 512, 320),
-         (4, 512, 256, 128), (4, 768, 128, 64), (4, 896, 128, 48)]
-GROUPS = [(0, 512, "v"), (512, 128, "s"), (640, 128, "s"), (768, 128, "s"), (896, 128, "s")]
+LOADS = [[0, 0, 1024, [[0, 512, 304], [512, 512, 304]]], [1, 0, 1024, [[0, 512, 304], [512, 512, 304]]], [2, 0, 512, [[0, 512, 304]]], [3, 0, 512, [[0, 512, 256]]], [4, 0, 512, [[0, 256, 64], [256, 256, 128]]], [2, 512, 512, [[0, 512, 512]]], [3, 512, 512, [[0, 256, 192], [256, 256, 128]]], [4, 512, 384, [[0, 256, 160], [256, 128, 64]]], [4, 896, 128, [[0, 128, 64]]]]
+GROUPS = [[0, 128, "s"], [128, 128, "v"], [256, 128, "s"], [384, 128, "s"], [512, 128, "s"], [640, 128, "v"], [768, 128, "v"], [896, 128, "s"]]
 SCATTERS = [(0, 512), (512, 512)]
-SMALL = [("words", 0), ("s0", 0), ("s1", 1), ("s2", 1), ("s3", 2), ("u", 2), ("offs", 3), ("g0", 4), ("g1", 11)]
+SMALL = [["words", 0], ["s0", 0], ["s1", 1], ["s2", 1], ["s3", 1], ["u", 1], ["offs", 2], ["g0", 4], ["g1", 8]]
 
 
 def tile_list_hscat_d_none_kernel(tc, x, w4_words, w4_scales, c, u, wgo, offs, out):
@@ -71,7 +69,7 @@ def tile_list_hscat_d_none_kernel(tc, x, w4_words, w4_scales, c, u, wgo, offs, o
                 nc.sync.dma_start(out=gains[i][:], in_=wgo[:, s0 : s0 + w])
 
         raws = []
-        for i, (a, c0, w, ws) in enumerate(LOADS):
+        for i, (a, c0, w, pieces) in enumerate(LOADS):
             rows = x[a * K_PASS : (a + 1) * K_PASS, :] if a < X_PASSES else c
             raw = keep.tile([P, PACK, w], F32, name="raw%d" % i)
             nc.sync.dma_start(out=raw[:], in_=rows[:, c0 : c0 + w].rearrange("(p j) w -> p j w", j=PACK))
@@ -86,12 +84,11 @@ def tile_list_hscat_d_none_kernel(tc, x, w4_words, w4_scales, c, u, wgo, offs, o
         done = [0 for g in GROUPS]
         emptied = [0 for s in SCATTERS]
 
-        for i, (a, c0, w, ws) in enumerate(LOADS):
+        for i, (a, c0, w, pieces) in enumerate(LOADS):
             grouped = keep.tile([P, w, PACK], BF16, name="grouped%d" % i, align_bytes=64)
             codes = keep.tile([P, w], U32, name="codes%d" % i, align_bytes=64)
             scales = keep.tile([P, w], U8, name="scales%d" % i, align_bytes=64)
-            for h0 in range(0, w, HALF):
-                hw = min(HALF, w)
+            for h0, hw, ws in pieces:
                 if ws > 0:
                     interleave(nc.scalar.copy, grouped, raws[i], h0, h0 + ws)
                 if ws < hw:
@@ -101,7 +98,7 @@ def tile_list_hscat_d_none_kernel(tc, x, w4_words, w4_scales, c, u, wgo, offs, o
                     scales=scales[:, h0 : h0 + hw],
                     in_=grouped[:, h0 : h0 + hw, :].rearrange("p w j -> p (w j)"),
                 )
-            if i == 3:
+            if i == 2:
                 u_grouped = keep.tile([P, M, PACK], BF16, name="u_grouped", align_bytes=64)
                 interleave(nc.vector.tensor_copy, u_grouped, u_raw, 0, M)
                 nc.vector.quantize_mx(

@@ -21,9 +21,10 @@ X_PASSES = K // K_PASS
 HALF = S // 2
 
 LOADS = [[0, 0, 1024, [[0, 512, 304], [512, 512, 304]]], [1, 0, 1024, [[0, 512, 304], [512, 512, 304]]], [2, 0, 512, [[0, 512, 304]]], [3, 0, 512, [[0, 512, 256]]], [4, 0, 512, [[0, 256, 64], [256, 256, 128]]], [2, 512, 512, [[0, 512, 512]]], [3, 512, 512, [[0, 256, 192], [256, 256, 128]]], [4, 512, 384, [[0, 256, 160], [256, 128, 64]]], [4, 896, 128, [[0, 128, 64]]]]
-GROUPS = [[0, 128, "s"], [128, 128, "v"], [256, 128, "s"], [384, 128, "s"], [512, 128, "s"], [640, 128, "v"], [768, 128, "v"], [896, 128, "s"]]
-SCATTERS = [(0, 512), (512, 512)]
-SMALL = [["words", 0], ["s0", 0], ["s1", 1], ["s2", 1], ["s3", 1], ["u", 1], ["offs", 2], ["g0", 4], ["g1", 8]]
+GROUPS = [[0, 128, "s"], [128, 128, "v"], [256, 128, "s"], [384, 128, "s"], [512, 128, "s"], [640, 128, "s"], [768, 128, "s"], [896, 128, "s"]]
+SCATTERS = [(0, 512), (512, 128), (640, 128), (768, 128), (896, 128)]
+GAINS = [(0, 512), (512, 512)]
+SMALL = [["words", 0], ["s0", 0], ["s1", 1], ["s2", 1], ["s3", 1], ["u", 1], ["offs", 2], ["g0", 4], ["g1", 6]]
 
 
 def tile_list_hscat_d_none_kernel(tc, x, w4_words, w4_scales, c, u, wgo, offs, out):
@@ -44,7 +45,7 @@ def tile_list_hscat_d_none_kernel(tc, x, w4_words, w4_scales, c, u, wgo, offs, o
         w_words = keep.tile([P, X_PASSES, 2 * M], U8, name="w_words", align_bytes=64)
         w_scales = keep.tile([P, X_PASSES, M], U8, name="w_scales", align_bytes=64)
         u_raw = keep.tile([P, PACK, M], F32, name="u_raw")
-        gains = [keep.tile([P, w], F32, name="gain%d" % i) for i, (s0, w) in enumerate(SCATTERS)]
+        gains = [keep.tile([P, w], F32, name="gain%d" % i) for i, (s0, w) in enumerate(GAINS)]
         sums = [keep.tile([P, w], F32, name="sum%d" % i) for i, (s0, w) in enumerate(SCATTERS)]
 
         nc.vector.memset(w_scales[:].rearrange("p a n -> p (a n)").bitcast(I32), 0)
@@ -65,7 +66,7 @@ def tile_list_hscat_d_none_kernel(tc, x, w4_words, w4_scales, c, u, wgo, offs, o
                 )
             else:
                 i = int(name[1])
-                s0, w = SCATTERS[i]
+                s0, w = GAINS[i]
                 nc.sync.dma_start(out=gains[i][:], in_=wgo[:, s0 : s0 + w])
 
         raws = []
@@ -128,7 +129,7 @@ def tile_list_hscat_d_none_kernel(tc, x, w4_words, w4_scales, c, u, wgo, offs, o
                         nc.vector.tensor_tensor(
                             window[:].indirect(offsets[:, s0 // 16 : (s0 + sw) // 16]),
                             sums[s][:],
-                            gains[s][:],
+                            gains[s0 // HALF][:, s0 % HALF : s0 % HALF + sw],
                             mybir.AluOpType.mult,
                         )
 

@@ -18,13 +18,14 @@ P = 128
 PACK = 4
 K_PASS = P * PACK
 X_PASSES = K // K_PASS
-HALF = S // 2
+PASSES = X_PASSES + 1
+GROUP = 128
 
-LOADS = [[0, 0, 1024, [[0, 512, 304], [512, 512, 304]]], [1, 0, 1024, [[0, 512, 304], [512, 512, 304]]], [2, 0, 512, [[0, 512, 304]]], [3, 0, 512, [[0, 512, 256]]], [4, 0, 512, [[0, 256, 64], [256, 256, 128]]], [2, 512, 512, [[0, 512, 512]]], [3, 512, 512, [[0, 256, 192], [256, 256, 128]]], [4, 512, 384, [[0, 256, 160], [256, 128, 64]]], [4, 896, 128, [[0, 128, 64]]]]
-GROUPS = [[0, 128, "s"], [128, 128, "v"], [256, 128, "s"], [384, 128, "s"], [512, 128, "s"], [640, 128, "s"], [768, 128, "s"], [896, 128, "s"]]
-SCATTERS = [(0, 512), (512, 128), (640, 128), (768, 128), (896, 128)]
-GAINS = [(0, 512), (512, 512)]
-SMALL = [["words", 0], ["s0", 0], ["s1", 1], ["s2", 1], ["s3", 1], ["u", 1], ["offs", 2], ["g0", 4], ["g1", 6]]
+FULL = 0
+WIDTHS = [256,256,256,128,128]
+PIECE = 512
+SHARE_EARLY, SHARE_LATE, SHARE_LAST = 10, 12, 6
+SMALL_PER_LOAD = 2
 
 
 def tile_list_hscat_d_none_kernel(tc, x, w4_words, w4_scales, c, u, wgo, offs, out):
@@ -36,6 +37,11 @@ def tile_list_hscat_d_none_kernel(tc, x, w4_words, w4_scales, c, u, wgo, offs, o
             in_=src[:, :, lo:hi].rearrange("p t (c i) -> p c t i", i=4),
         )
 
+    starts = [sum(WIDTHS[:i]) for i in range(len(WIDTHS))]
+    loads = [(a, 0, S, -1) for a in range(FULL)]
+    for i, w in enumerate(WIDTHS):
+        loads.extend((a, starts[i], w, i) for a in range(FULL, PASSES))
+
     with ExitStack() as ctx:
         keep = ctx.enter_context(tc.tile_pool(name="keep", bufs=1))
         psum = ctx.enter_context(tc.psum_pool(name="psum", bufs=1))
@@ -45,51 +51,56 @@ def tile_list_hscat_d_none_kernel(tc, x, w4_words, w4_scales, c, u, wgo, offs, o
         w_words = keep.tile([P, X_PASSES, 2 * M], U8, name="w_words", align_bytes=64)
         w_scales = keep.tile([P, X_PASSES, M], U8, name="w_scales", align_bytes=64)
         u_raw = keep.tile([P, PACK, M], F32, name="u_raw")
-        gains = [keep.tile([P, w], F32, name="gain%d" % i) for i, (s0, w) in enumerate(GAINS)]
-        sums = [keep.tile([P, w], F32, name="sum%d" % i) for i, (s0, w) in enumerate(SCATTERS)]
+        gains = [keep.tile([P, w], F32, name="gain%d" % i) for i, w in enumerate(WIDTHS)]
+        sums = [keep.tile([P, w], F32, name="sum%d" % i) for i, w in enumerate(WIDTHS)]
 
         nc.vector.memset(w_scales[:].rearrange("p a n -> p (a n)").bitcast(I32), 0)
         nc.vector.memset(window[:], 0.0)
 
-        def small_load(name):
-            if name == "offs":
-                nc.sync.dma_start(offsets[:], offs)
-            elif name == "words":
-                nc.sync.dma_start(out=w_words[:].bitcast(I32), in_=w4_words.rearrange("a p b -> p a b").bitcast(I32))
-            elif name == "u":
-                nc.sync.dma_start(out=u_raw[:], in_=u.rearrange("(p j) n -> p j n", j=PACK))
-            elif name[0] == "s":
-                q = int(name[1])
-                nc.sync.dma_start(
-                    out=w_scales[32 * q : 32 * q + 4, :, :].bitcast(I32),
-                    in_=w4_scales[:, 4 * q : 4 * q + 4, :].rearrange("a r n -> r a n").bitcast(I32),
-                )
-            else:
-                i = int(name[1])
-                s0, w = GAINS[i]
-                nc.sync.dma_start(out=gains[i][:], in_=wgo[:, s0 : s0 + w])
+        def scale_load(q):
+            nc.sync.dma_start(
+                out=w_scales[32 * q : 32 * q + 4, :, :].bitcast(I32),
+                in_=w4_scales[:, 4 * q : 4 * q + 4, :].rearrange("a r n -> r a n").bitcast(I32),
+            )
+
+        small = [
+            lambda: nc.sync.dma_start(
+                out=w_words[:].bitcast(I32), in_=w4_words.rearrange("a p b -> p a b").bitcast(I32)
+            ),
+            lambda: nc.sync.dma_start(out=u_raw[:], in_=u.rearrange("(p j) n -> p j n", j=PACK)),
+            lambda: scale_load(0),
+            lambda: scale_load(1),
+            lambda: scale_load(2),
+            lambda: scale_load(3),
+            lambda: nc.sync.dma_start(offsets[:], offs),
+        ]
 
         raws = []
-        for i, (a, c0, w, pieces) in enumerate(LOADS):
+        for i, (a, c0, w, chunk) in enumerate(loads):
             rows = x[a * K_PASS : (a + 1) * K_PASS, :] if a < X_PASSES else c
             raw = keep.tile([P, PACK, w], F32, name="raw%d" % i)
             nc.sync.dma_start(out=raw[:], in_=rows[:, c0 : c0 + w].rearrange("(p j) w -> p j w", j=PACK))
             raws.append(raw)
-            for name, at in SMALL:
-                if at == i:
-                    small_load(name)
+            for load in small[i * SMALL_PER_LOAD : (i + 1) * SMALL_PER_LOAD]:
+                load()
+            if a == PASSES - 1:
+                nc.sync.dma_start(out=gains[chunk][:], in_=wgo[:, c0 : c0 + w])
 
         u_codes = keep.tile([P, M], U32, name="u_codes", align_bytes=64)
         u_scales = keep.tile([P, M], U8, name="u_scales", align_bytes=64)
-        banks = [psum.tile([P, w], F32, name="bank%d" % g) for g, (g0, w, e) in enumerate(GROUPS)]
-        done = [0 for g in GROUPS]
-        emptied = [0 for s in SCATTERS]
+        banks = [psum.tile([P, GROUP], F32, name="bank%d" % g) for g in range(S // GROUP)]
 
-        for i, (a, c0, w, pieces) in enumerate(LOADS):
+        for i, (a, c0, w, chunk) in enumerate(loads):
             grouped = keep.tile([P, w, PACK], BF16, name="grouped%d" % i, align_bytes=64)
             codes = keep.tile([P, w], U32, name="codes%d" % i, align_bytes=64)
             scales = keep.tile([P, w], U8, name="scales%d" % i, align_bytes=64)
-            for h0, hw, ws in pieces:
+            share = SHARE_EARLY if chunk <= 0 else SHARE_LATE
+            if i == len(loads) - 1:
+                share = SHARE_LAST
+            h0 = 0
+            while h0 < w:
+                hw = max(v for v in (128, 256, 512) if v <= min(PIECE, w - h0))
+                ws = hw * share // 16
                 if ws > 0:
                     interleave(nc.scalar.copy, grouped, raws[i], h0, h0 + ws)
                 if ws < hw:
@@ -99,38 +110,33 @@ def tile_list_hscat_d_none_kernel(tc, x, w4_words, w4_scales, c, u, wgo, offs, o
                     scales=scales[:, h0 : h0 + hw],
                     in_=grouped[:, h0 : h0 + hw, :].rearrange("p w j -> p (w j)"),
                 )
-            if i == 2:
+                h0 += hw
+            if i == 1:
                 u_grouped = keep.tile([P, M, PACK], BF16, name="u_grouped", align_bytes=64)
                 interleave(nc.vector.tensor_copy, u_grouped, u_raw, 0, M)
                 nc.vector.quantize_mx(
                     out=u_codes[:].bitcast(FP8X4), scales=u_scales[:], in_=u_grouped[:].rearrange("p w j -> p (w j)")
                 )
-            for g, (g0, gw, eng) in enumerate(GROUPS):
-                if g0 < c0 or g0 + gw > c0 + w:
-                    continue
-                cols = slice(g0 - c0, g0 - c0 + gw)
+            for g0 in range(c0, c0 + w, GROUP):
+                cols = slice(g0 - c0, g0 - c0 + GROUP)
+                bank = banks[g0 // GROUP]
                 nc.tensor.matmul_mx(
-                    out=banks[g][:],
+                    out=bank[:],
                     lhsT=w_words[:, a, :].bitcast(FP4X4) if a < X_PASSES else u_codes[:].bitcast(FP8X4),
                     lhsT_scale=w_scales[:, a, :] if a < X_PASSES else u_scales[:],
                     rhs=codes[:, cols].bitcast(FP8X4),
                     rhs_scale=scales[:, cols],
-                    start=(done[g] == 0),
-                    stop=(done[g] == X_PASSES),
+                    start=(a == 0),
+                    stop=(a == PASSES - 1),
                 )
-                done[g] += 1
-                if done[g] == X_PASSES + 1:
-                    s = [k for k, (s0, sw) in enumerate(SCATTERS) if s0 <= g0 < s0 + sw][0]
-                    s0, sw = SCATTERS[s]
-                    copy = nc.vector.tensor_copy if eng == "v" else nc.scalar.copy
-                    copy(out=sums[s][:, g0 - s0 : g0 - s0 + gw], in_=banks[g][:])
-                    emptied[s] += gw
-                    if emptied[s] == sw:
-                        nc.vector.tensor_tensor(
-                            window[:].indirect(offsets[:, s0 // 16 : (s0 + sw) // 16]),
-                            sums[s][:],
-                            gains[s0 // HALF][:, s0 % HALF : s0 % HALF + sw],
-                            mybir.AluOpType.mult,
-                        )
+                if a == PASSES - 1:
+                    nc.scalar.copy(out=sums[chunk][:, cols], in_=bank[:])
+            if a == PASSES - 1:
+                nc.vector.tensor_tensor(
+                    window[:].indirect(offsets[:, c0 // 16 : (c0 + w) // 16]),
+                    sums[chunk][:],
+                    gains[chunk][:],
+                    mybir.AluOpType.mult,
+                )
 
         nc.sync.dma_start(out=out, in_=window[:])

@@ -1,6 +1,7 @@
 from contextlib import ExitStack
 
 import concourse.mybir as mybir
+from concourse.masks import make_identity
 
 K, M, T, S, L = 2048, 128, 2048, 1024, 512
 FLOPS = 2 * (K + L) * M * S
@@ -21,10 +22,13 @@ X_PASSES = K // K_PASS
 PASSES = X_PASSES + 1
 GROUP = 128
 
-FULL = 0
-WIDTHS = [256,256,256,128,128]
-PIECE = 512
-SHARE_EARLY, SHARE_LATE, SHARE_LAST = 10, 12, 6
+WIDTHS = [[512,256,256],[512,256,256],[512,256,256],[512,256,256],[512,256,256]]
+SCATTERS = [512,256,256]
+EMPTY = "ssv"
+PIECE, PIECE_LAST = 256, 256
+SPREAD = "s"
+HEADS = 8
+SHARE_EARLY, SHARE_LATE, SHARE_LAST = 6, 16, 4
 SMALL_PER_LOAD = 2
 
 
@@ -37,10 +41,13 @@ def tile_list_hscat_d_none_kernel(tc, x, w4_words, w4_scales, c, u, wgo, offs, o
             in_=src[:, :, lo:hi].rearrange("p t (c i) -> p c t i", i=4),
         )
 
-    starts = [sum(WIDTHS[:i]) for i in range(len(WIDTHS))]
-    loads = [(a, 0, S, -1) for a in range(FULL)]
-    for i, w in enumerate(WIDTHS):
-        loads.extend((a, starts[i], w, i) for a in range(FULL, PASSES))
+    def spans(widths):
+        return [(sum(widths[:i]), w) for i, w in enumerate(widths)]
+
+    loads = sorted((c0, a, w) for a in range(PASSES) for c0, w in spans(WIDTHS[a]))
+    loads = [(a, c0, w) for c0, a, w in loads]
+    scatters = spans(SCATTERS)
+    first_done = [i for i, (a, c0, w) in enumerate(loads) if a == X_PASSES and c0 + w >= SCATTERS[0]][0]
 
     with ExitStack() as ctx:
         keep = ctx.enter_context(tc.tile_pool(name="keep", bufs=1))
@@ -51,11 +58,16 @@ def tile_list_hscat_d_none_kernel(tc, x, w4_words, w4_scales, c, u, wgo, offs, o
         w_words = keep.tile([P, X_PASSES, 2 * M], U8, name="w_words", align_bytes=64)
         w_scales = keep.tile([P, X_PASSES, M], U8, name="w_scales", align_bytes=64)
         u_raw = keep.tile([P, PACK, M], F32, name="u_raw")
-        gains = [keep.tile([P, w], F32, name="gain%d" % i) for i, w in enumerate(WIDTHS)]
-        sums = [keep.tile([P, w], F32, name="sum%d" % i) for i, w in enumerate(WIDTHS)]
+        gains = keep.tile([P, S], F32, name="gains")
+        head_rows = keep.tile([P, S], F32, name="head_rows")
+        spread = keep.tile([P, S], F32, name="spread")
+        ident = keep.tile([P, P], F32, name="ident")
+        sums = [keep.tile([P, w], F32, name="sum%d" % i) for i, w in enumerate(SCATTERS)]
 
         nc.vector.memset(w_scales[:].rearrange("p a n -> p (a n)").bitcast(I32), 0)
+        nc.gpsimd.memset(head_rows[:], 0.0)
         nc.vector.memset(window[:], 0.0)
+        make_identity(nc, ident[:])
 
         def scale_load(q):
             nc.sync.dma_start(
@@ -64,6 +76,7 @@ def tile_list_hscat_d_none_kernel(tc, x, w4_words, w4_scales, c, u, wgo, offs, o
             )
 
         small = [
+            lambda: nc.sync.dma_start(out=head_rows[0:P:16, :], in_=wgo[0:P:16, :]),
             lambda: nc.sync.dma_start(
                 out=w_words[:].bitcast(I32), in_=w4_words.rearrange("a p b -> p a b").bitcast(I32)
             ),
@@ -76,30 +89,45 @@ def tile_list_hscat_d_none_kernel(tc, x, w4_words, w4_scales, c, u, wgo, offs, o
         ]
 
         raws = []
-        for i, (a, c0, w, chunk) in enumerate(loads):
+        for i, (a, c0, w) in enumerate(loads):
             rows = x[a * K_PASS : (a + 1) * K_PASS, :] if a < X_PASSES else c
             raw = keep.tile([P, PACK, w], F32, name="raw%d" % i)
             nc.sync.dma_start(out=raw[:], in_=rows[:, c0 : c0 + w].rearrange("(p j) w -> p j w", j=PACK))
             raws.append(raw)
             for load in small[i * SMALL_PER_LOAD : (i + 1) * SMALL_PER_LOAD]:
                 load()
-            if a == PASSES - 1:
-                nc.sync.dma_start(out=gains[chunk][:], in_=wgo[:, c0 : c0 + w])
+
+        spread_copy = nc.scalar.copy if SPREAD == "s" else nc.vector.tensor_copy
+        for h in range(2):
+            turned = psum.tile([P, 4, P], F32, name="turned%d" % h, tag="bank%d" % (4 + h))
+            for b in range(4):
+                c0 = (4 * h + b) * P
+                nc.tensor.transpose(turned[:, b, :], head_rows[:, c0 : c0 + P], ident[:])
+            spread_copy(
+                out=spread[:, 512 * h : 512 * (h + 1)].rearrange("p (b g r) -> p b g r", b=4, g=HEADS),
+                in_=turned[:, :, 0:P:16].unsqueeze(3).to_broadcast([P, 4, HEADS, 16]),
+            )
+        for h in range(2):
+            back = psum.tile([P, 4, P], F32, name="back%d" % h, tag="bank%d" % (6 + h))
+            for b in range(4):
+                c0 = (4 * h + b) * P
+                nc.tensor.transpose(back[:, b, :], spread[:, c0 : c0 + P], ident[:])
+            spread_copy(out=gains[:, 512 * h : 512 * (h + 1)], in_=back[:].rearrange("p b n -> p (b n)"))
 
         u_codes = keep.tile([P, M], U32, name="u_codes", align_bytes=64)
         u_scales = keep.tile([P, M], U8, name="u_scales", align_bytes=64)
-        banks = [psum.tile([P, GROUP], F32, name="bank%d" % g) for g in range(S // GROUP)]
+        banks = [psum.tile([P, GROUP], F32, name="bank%d" % g, tag="bank%d" % g) for g in range(S // GROUP)]
 
-        for i, (a, c0, w, chunk) in enumerate(loads):
+        for i, (a, c0, w) in enumerate(loads):
             grouped = keep.tile([P, w, PACK], BF16, name="grouped%d" % i, align_bytes=64)
             codes = keep.tile([P, w], U32, name="codes%d" % i, align_bytes=64)
             scales = keep.tile([P, w], U8, name="scales%d" % i, align_bytes=64)
-            share = SHARE_EARLY if chunk <= 0 else SHARE_LATE
+            share = SHARE_EARLY if i <= first_done else SHARE_LATE
             if i == len(loads) - 1:
                 share = SHARE_LAST
             h0 = 0
             while h0 < w:
-                hw = max(v for v in (128, 256, 512) if v <= min(PIECE, w - h0))
+                hw = max(v for v in (128, 256, 512) if v <= min(PIECE_LAST if a == X_PASSES else PIECE, w - h0))
                 ws = hw * share // 16
                 if ws > 0:
                     interleave(nc.scalar.copy, grouped, raws[i], h0, h0 + ws)
@@ -129,14 +157,17 @@ def tile_list_hscat_d_none_kernel(tc, x, w4_words, w4_scales, c, u, wgo, offs, o
                     start=(a == 0),
                     stop=(a == PASSES - 1),
                 )
-                if a == PASSES - 1:
-                    nc.scalar.copy(out=sums[chunk][:, cols], in_=bank[:])
-            if a == PASSES - 1:
-                nc.vector.tensor_tensor(
-                    window[:].indirect(offsets[:, c0 // 16 : (c0 + w) // 16]),
-                    sums[chunk][:],
-                    gains[chunk][:],
-                    mybir.AluOpType.mult,
-                )
+                if a == X_PASSES:
+                    s = [j for j, (s0, sw) in enumerate(scatters) if s0 <= g0 < s0 + sw][0]
+                    s0, sw = scatters[s]
+                    empty = nc.scalar.copy if EMPTY[s] == "s" else nc.vector.tensor_copy
+                    empty(out=sums[s][:, g0 - s0 : g0 - s0 + GROUP], in_=bank[:])
+                    if g0 + GROUP == s0 + sw:
+                        nc.vector.tensor_tensor(
+                            window[:].indirect(offsets[:, s0 // 16 : (s0 + sw) // 16]),
+                            sums[s][:],
+                            gains[:, s0 : s0 + sw],
+                            mybir.AluOpType.mult,
+                        )
 
         nc.sync.dma_start(out=out, in_=window[:])

@@ -22,13 +22,14 @@ X_PASSES = K // K_PASS
 PASSES = X_PASSES + 1
 GROUP = 128
 
-WIDTHS = [[512,256,256],[512,256,256],[512,256,256],[512,256,256],[512,256,256]]
+WIDTHS = [[512,256,256],[512,256,256],[512,256,256],[512,256,256],[512,256,128,128]]
 SCATTERS = [512,256,256]
-EMPTY = "ssv"
-PIECE, PIECE_LAST = 256, 256
+EMPTY = "vvvvv"
+PIECE, PIECE_LAST = 512, 256
 SPREAD = "s"
 HEADS = 8
-SHARE_EARLY, SHARE_LATE, SHARE_LAST = 6, 16, 4
+SOLO = [1,4]
+SHARE_EARLY, SHARE_LATE, SHARE_LAST = 4, 8, 8
 SMALL_PER_LOAD = 2
 
 
@@ -123,7 +124,9 @@ def tile_list_hscat_d_none_kernel(tc, x, w4_words, w4_scales, c, u, wgo, offs, o
             codes = keep.tile([P, w], U32, name="codes%d" % i, align_bytes=64)
             scales = keep.tile([P, w], U8, name="scales%d" % i, align_bytes=64)
             share = SHARE_EARLY if i <= first_done else SHARE_LATE
-            if i == len(loads) - 1:
+            if i > first_done and SOLO[0] <= a < SOLO[1]:
+                share = 16
+            if i > first_done and a == X_PASSES:
                 share = SHARE_LAST
             h0 = 0
             while h0 < w:

@@ -22,15 +22,17 @@ X_PASSES = K // K_PASS
 PASSES = X_PASSES + 1
 GROUP = 128
 
-WIDTHS = [[512,256,256],[512,256,256],[512,256,256],[512,256,256],[512,256,128,128]]
+WIDTHS = [[1024],[1024],[512,512],[512,256,256],[512,256,256]]
 SCATTERS = [512,256,256]
-EMPTY = "vvvvv"
-PIECE, PIECE_LAST = 512, 256
+EMPTY = "mss"
+PIECE, PIECE_LAST = 256, 256
 SPREAD = "s"
 HEADS = 8
-SOLO = [1,4]
-SHARE_EARLY, SHARE_LATE, SHARE_LAST = 4, 8, 8
-SMALL_PER_LOAD = 2
+U_AT = 3
+SHARES = [8,8,8,8,6,16,16,16,16,0]
+HOLD = [-1,8,-1]
+POOL = [0,0,0,0,0,0,0,0,0,0]
+SMALL_AT = [0,1,1,1,1,0,2,4]
 
 
 def tile_list_hscat_d_none_kernel(tc, x, w4_words, w4_scales, c, u, wgo, offs, out):
@@ -63,7 +65,6 @@ def tile_list_hscat_d_none_kernel(tc, x, w4_words, w4_scales, c, u, wgo, offs, o
         head_rows = keep.tile([P, S], F32, name="head_rows")
         spread = keep.tile([P, S], F32, name="spread")
         ident = keep.tile([P, P], F32, name="ident")
-        sums = [keep.tile([P, w], F32, name="sum%d" % i) for i, w in enumerate(SCATTERS)]
 
         nc.vector.memset(w_scales[:].rearrange("p a n -> p (a n)").bitcast(I32), 0)
         nc.gpsimd.memset(head_rows[:], 0.0)
@@ -77,26 +78,27 @@ def tile_list_hscat_d_none_kernel(tc, x, w4_words, w4_scales, c, u, wgo, offs, o
             )
 
         small = [
-            lambda: nc.sync.dma_start(out=head_rows[0:P:16, :], in_=wgo[0:P:16, :]),
             lambda: nc.sync.dma_start(
                 out=w_words[:].bitcast(I32), in_=w4_words.rearrange("a p b -> p a b").bitcast(I32)
             ),
-            lambda: nc.sync.dma_start(out=u_raw[:], in_=u.rearrange("(p j) n -> p j n", j=PACK)),
             lambda: scale_load(0),
             lambda: scale_load(1),
             lambda: scale_load(2),
             lambda: scale_load(3),
+            lambda: nc.sync.dma_start(out=head_rows[0:P:16, :], in_=wgo[0:P:16, :]),
+            lambda: nc.sync.dma_start(out=u_raw[:], in_=u.rearrange("(p j) n -> p j n", j=PACK)),
             lambda: nc.sync.dma_start(offsets[:], offs),
         ]
 
         raws = []
         for i, (a, c0, w) in enumerate(loads):
             rows = x[a * K_PASS : (a + 1) * K_PASS, :] if a < X_PASSES else c
-            raw = keep.tile([P, PACK, w], F32, name="raw%d" % i)
+            raw = keep.tile([P, PACK, w], F32, name="raw%d" % i, tag="raw%d" % i)
             nc.sync.dma_start(out=raw[:], in_=rows[:, c0 : c0 + w].rearrange("(p j) w -> p j w", j=PACK))
             raws.append(raw)
-            for load in small[i * SMALL_PER_LOAD : (i + 1) * SMALL_PER_LOAD]:
-                load()
+            for load, at in zip(small, SMALL_AT):
+                if at == i:
+                    load()
 
         spread_copy = nc.scalar.copy if SPREAD == "s" else nc.vector.tensor_copy
         for h in range(2):
@@ -119,58 +121,67 @@ def tile_list_hscat_d_none_kernel(tc, x, w4_words, w4_scales, c, u, wgo, offs, o
         u_scales = keep.tile([P, M], U8, name="u_scales", align_bytes=64)
         banks = [psum.tile([P, GROUP], F32, name="bank%d" % g, tag="bank%d" % g) for g in range(S // GROUP)]
 
+        def place(s, tag):
+            s0, sw = scatters[s]
+            sums = keep.tile([P, sw], F32, name="sum%d" % s, tag=tag)
+            for g0 in range(s0, s0 + sw, GROUP):
+                part = sums[:, g0 - s0 : g0 - s0 + GROUP]
+                if EMPTY[s] == "m":
+                    nc.vector.tensor_tensor(part, banks[g0 // GROUP][:], gains[:, g0 : g0 + GROUP], mybir.AluOpType.mult)
+                elif EMPTY[s] == "s":
+                    nc.scalar.copy(out=part, in_=banks[g0 // GROUP][:])
+                else:
+                    nc.vector.tensor_copy(out=part, in_=banks[g0 // GROUP][:])
+            places = window[:].indirect(offsets[:, s0 // 16 : (s0 + sw) // 16])
+            if EMPTY[s] == "m":
+                nc.vector.tensor_copy(out=places, in_=sums[:])
+            else:
+                nc.vector.tensor_tensor(places, sums[:], gains[:, s0 : s0 + sw], mybir.AluOpType.mult)
+
         for i, (a, c0, w) in enumerate(loads):
             grouped = keep.tile([P, w, PACK], BF16, name="grouped%d" % i, align_bytes=64)
             codes = keep.tile([P, w], U32, name="codes%d" % i, align_bytes=64)
             scales = keep.tile([P, w], U8, name="scales%d" % i, align_bytes=64)
-            share = SHARE_EARLY if i <= first_done else SHARE_LATE
-            if i > first_done and SOLO[0] <= a < SOLO[1]:
-                share = 16
-            if i > first_done and a == X_PASSES:
-                share = SHARE_LAST
+            share = SHARES[i]
             h0 = 0
             while h0 < w:
                 hw = max(v for v in (128, 256, 512) if v <= min(PIECE_LAST if a == X_PASSES else PIECE, w - h0))
-                ws = hw * share // 16
+                wg = hw * POOL[i] // 16
+                ws = min(hw - wg, hw * share // 16)
                 if ws > 0:
                     interleave(nc.scalar.copy, grouped, raws[i], h0, h0 + ws)
-                if ws < hw:
-                    interleave(nc.vector.tensor_copy, grouped, raws[i], h0 + ws, h0 + hw)
+                if wg > 0:
+                    interleave(nc.gpsimd.tensor_copy, grouped, raws[i], h0 + ws, h0 + ws + wg)
+                if ws + wg < hw:
+                    interleave(nc.vector.tensor_copy, grouped, raws[i], h0 + ws + wg, h0 + hw)
                 nc.vector.quantize_mx(
                     out=codes[:, h0 : h0 + hw].bitcast(FP8X4),
                     scales=scales[:, h0 : h0 + hw],
                     in_=grouped[:, h0 : h0 + hw, :].rearrange("p w j -> p (w j)"),
                 )
                 h0 += hw
-            if i == 1:
+            if i == U_AT:
                 u_grouped = keep.tile([P, M, PACK], BF16, name="u_grouped", align_bytes=64)
                 interleave(nc.vector.tensor_copy, u_grouped, u_raw, 0, M)
                 nc.vector.quantize_mx(
                     out=u_codes[:].bitcast(FP8X4), scales=u_scales[:], in_=u_grouped[:].rearrange("p w j -> p (w j)")
                 )
+            for s in range(len(scatters)):
+                if HOLD[s] == i:
+                    place(s, "raw%d" % i)
             for g0 in range(c0, c0 + w, GROUP):
                 cols = slice(g0 - c0, g0 - c0 + GROUP)
-                bank = banks[g0 // GROUP]
                 nc.tensor.matmul_mx(
-                    out=bank[:],
+                    out=banks[g0 // GROUP][:],
                     lhsT=w_words[:, a, :].bitcast(FP4X4) if a < X_PASSES else u_codes[:].bitcast(FP8X4),
                     lhsT_scale=w_scales[:, a, :] if a < X_PASSES else u_scales[:],
                     rhs=codes[:, cols].bitcast(FP8X4),
                     rhs_scale=scales[:, cols],
                     start=(a == 0),
-                    stop=(a == PASSES - 1),
+                    stop=(a == X_PASSES),
                 )
-                if a == X_PASSES:
-                    s = [j for j, (s0, sw) in enumerate(scatters) if s0 <= g0 < s0 + sw][0]
-                    s0, sw = scatters[s]
-                    empty = nc.scalar.copy if EMPTY[s] == "s" else nc.vector.tensor_copy
-                    empty(out=sums[s][:, g0 - s0 : g0 - s0 + GROUP], in_=bank[:])
-                    if g0 + GROUP == s0 + sw:
-                        nc.vector.tensor_tensor(
-                            window[:].indirect(offsets[:, s0 // 16 : (s0 + sw) // 16]),
-                            sums[s][:],
-                            gains[:, s0 : s0 + sw],
-                            mybir.AluOpType.mult,
-                        )
+            for s, (s0, sw) in enumerate(scatters):
+                if a == X_PASSES and c0 < s0 + sw <= c0 + w and HOLD[s] < 0:
+                    place(s, "sum%d" % s)
 
         nc.sync.dma_start(out=out, in_=window[:])

@@ -22,17 +22,17 @@ X_PASSES = K // K_PASS
 PASSES = X_PASSES + 1
 GROUP = 128
 
-WIDTHS = [[1024],[1024],[512,512],[512,256,256],[512,256,256]]
-SCATTERS = [512,256,256]
-EMPTY = "mss"
-PIECE, PIECE_LAST = 256, 256
+WIDTHS = [[1024],[1024],[1024],[256,256,256,256],[256,256,256,256]]
+SCATTERS = [256,256,256,256]
+EMPTY = "ssss"
+PIECE, PIECE_LAST = 512, 256
 SPREAD = "s"
 HEADS = 8
-U_AT = 3
-SHARES = [8,8,8,8,6,16,16,16,16,0]
-HOLD = [-1,8,-1]
-POOL = [0,0,0,0,0,0,0,0,0,0]
-SMALL_AT = [0,1,1,1,1,0,2,4]
+U_AT = 1
+SHARES = [6,6,6,6,6,6,16,16,6,16,6]
+HOLD = [5,7,9,-1]
+POOL = [0,0,0,0,0,0,0,0,0,0,0]
+SMALL_AT = [0,1,1,1,1,0,0,4]
 
 
 def tile_list_hscat_d_none_kernel(tc, x, w4_words, w4_scales, c, u, wgo, offs, out):

@@ -19,20 +19,16 @@ P = 128
 PACK = 4
 K_PASS = P * PACK
 X_PASSES = K // K_PASS
-PASSES = X_PASSES + 1
-GROUP = 128
+C_PASS = X_PASSES
+LIST_ROWS = 16
+LISTS = P // LIST_ROWS
+BANK_COLUMNS = 128
+BANK_WORDS = 512
 
-WIDTHS = [[1024],[1024],[1024],[256,256,256,256],[256,256,256,256]]
-SCATTERS = [256,256,256,256]
-EMPTY = "ssss"
-PIECE, PIECE_LAST = 512, 256
-SPREAD = "s"
-HEADS = 8
-U_AT = 1
-SHARES = [6,6,6,6,6,6,16,16,6,16,6]
-HOLD = [5,7,9,-1]
-POOL = [0,0,0,0,0,0,0,0,0,0,0]
-SMALL_AT = [0,1,1,1,1,0,0,4]
+FULL_PASSES = 3
+QUARTER = S // 4
+QUANTISE_COLUMNS = 512
+SCALAR_SIXTEENTHS = 6
 
 
 def tile_list_hscat_d_none_kernel(tc, x, w4_words, w4_scales, c, u, wgo, offs, out):
@@ -44,144 +40,121 @@ def tile_list_hscat_d_none_kernel(tc, x, w4_words, w4_scales, c, u, wgo, offs, o
             in_=src[:, :, lo:hi].rearrange("p t (c i) -> p c t i", i=4),
         )
 
-    def spans(widths):
-        return [(sum(widths[:i]), w) for i, w in enumerate(widths)]
+    def quantise(codes, scales, grouped):
+        nc.vector.quantize_mx(out=codes.bitcast(FP8X4), scales=scales, in_=grouped.rearrange("p w t -> p (w t)"))
 
-    loads = sorted((c0, a, w) for a in range(PASSES) for c0, w in spans(WIDTHS[a]))
-    loads = [(a, c0, w) for c0, a, w in loads]
-    scatters = spans(SCATTERS)
-    first_done = [i for i, (a, c0, w) in enumerate(loads) if a == X_PASSES and c0 + w >= SCATTERS[0]][0]
+    loads = [(a, 0, S) for a in range(FULL_PASSES)]
+    for first in range(0, S, QUARTER):
+        loads.extend((a, first, QUARTER) for a in range(FULL_PASSES, C_PASS + 1))
+    scalar_alone = [(C_PASS, QUARTER), (C_PASS - 1, 2 * QUARTER), (C_PASS - 1, 3 * QUARTER)]
 
     with ExitStack() as ctx:
         keep = ctx.enter_context(tc.tile_pool(name="keep", bufs=1))
         psum = ctx.enter_context(tc.psum_pool(name="psum", bufs=1))
 
-        offsets = keep.tile([P, S // 16], U16, name="offsets")
+        offsets = keep.tile([P, S // LIST_ROWS], U16, name="offsets")
         window = keep.tile([P, T], F32, name="window")
         w_words = keep.tile([P, X_PASSES, 2 * M], U8, name="w_words", align_bytes=64)
         w_scales = keep.tile([P, X_PASSES, M], U8, name="w_scales", align_bytes=64)
         u_raw = keep.tile([P, PACK, M], F32, name="u_raw")
         gains = keep.tile([P, S], F32, name="gains")
-        head_rows = keep.tile([P, S], F32, name="head_rows")
+        list_gains = keep.tile([P, S], F32, name="list_gains")
         spread = keep.tile([P, S], F32, name="spread")
         ident = keep.tile([P, P], F32, name="ident")
 
         nc.vector.memset(w_scales[:].rearrange("p a n -> p (a n)").bitcast(I32), 0)
-        nc.gpsimd.memset(head_rows[:], 0.0)
+        nc.gpsimd.memset(list_gains[:], 0.0)
         nc.vector.memset(window[:], 0.0)
         make_identity(nc, ident[:])
 
-        def scale_load(q):
-            nc.sync.dma_start(
+        nc.scalar.dma_start(out=w_words[:].bitcast(I32), in_=w4_words.rearrange("a p b -> p a b").bitcast(I32))
+        for q in range(4):
+            nc.scalar.dma_start(
                 out=w_scales[32 * q : 32 * q + 4, :, :].bitcast(I32),
                 in_=w4_scales[:, 4 * q : 4 * q + 4, :].rearrange("a r n -> r a n").bitcast(I32),
             )
-
-        small = [
-            lambda: nc.sync.dma_start(
-                out=w_words[:].bitcast(I32), in_=w4_words.rearrange("a p b -> p a b").bitcast(I32)
-            ),
-            lambda: scale_load(0),
-            lambda: scale_load(1),
-            lambda: scale_load(2),
-            lambda: scale_load(3),
-            lambda: nc.sync.dma_start(out=head_rows[0:P:16, :], in_=wgo[0:P:16, :]),
-            lambda: nc.sync.dma_start(out=u_raw[:], in_=u.rearrange("(p j) n -> p j n", j=PACK)),
-            lambda: nc.sync.dma_start(offsets[:], offs),
-        ]
+        nc.scalar.dma_start(out=list_gains[0:P:LIST_ROWS, :], in_=wgo[0:P:LIST_ROWS, :])
 
         raws = []
-        for i, (a, c0, w) in enumerate(loads):
-            rows = x[a * K_PASS : (a + 1) * K_PASS, :] if a < X_PASSES else c
-            raw = keep.tile([P, PACK, w], F32, name="raw%d" % i, tag="raw%d" % i)
-            nc.sync.dma_start(out=raw[:], in_=rows[:, c0 : c0 + w].rearrange("(p j) w -> p j w", j=PACK))
+        for i, (a, first, width) in enumerate(loads):
+            rows = c if a == C_PASS else x[a * K_PASS : (a + 1) * K_PASS, :]
+            raw = keep.tile([P, PACK, width], F32, name="raw%d" % i, tag="raw%d" % i)
+            nc.sync.dma_start(out=raw[:], in_=rows[:, first : first + width].rearrange("(p t) w -> p t w", t=PACK))
             raws.append(raw)
-            for load, at in zip(small, SMALL_AT):
-                if at == i:
-                    load()
+            if a == 1:
+                nc.sync.dma_start(out=u_raw[:], in_=u.rearrange("(p t) n -> p t n", t=PACK))
+            if a == C_PASS and first == 0:
+                nc.sync.dma_start(offsets[:], offs)
 
-        spread_copy = nc.scalar.copy if SPREAD == "s" else nc.vector.tensor_copy
-        for h in range(2):
-            turned = psum.tile([P, 4, P], F32, name="turned%d" % h, tag="bank%d" % (4 + h))
-            for b in range(4):
-                c0 = (4 * h + b) * P
-                nc.tensor.transpose(turned[:, b, :], head_rows[:, c0 : c0 + P], ident[:])
-            spread_copy(
-                out=spread[:, 512 * h : 512 * (h + 1)].rearrange("p (b g r) -> p b g r", b=4, g=HEADS),
-                in_=turned[:, :, 0:P:16].unsqueeze(3).to_broadcast([P, 4, HEADS, 16]),
+        blocks = BANK_WORDS // P
+        for h in range(S // BANK_WORDS):
+            turned = psum.tile([P, blocks, P], F32, name="turned%d" % h, tag="bank%d" % (4 + h))
+            for b in range(blocks):
+                j0 = (blocks * h + b) * P
+                nc.tensor.transpose(turned[:, b, :], list_gains[:, j0 : j0 + P], ident[:])
+            nc.scalar.copy(
+                out=spread[:, BANK_WORDS * h : BANK_WORDS * (h + 1)].rearrange(
+                    "p (b g r) -> p b g r", b=blocks, g=LISTS
+                ),
+                in_=turned[:, :, 0:P:LIST_ROWS].unsqueeze(3).to_broadcast([P, blocks, LISTS, LIST_ROWS]),
             )
-        for h in range(2):
-            back = psum.tile([P, 4, P], F32, name="back%d" % h, tag="bank%d" % (6 + h))
-            for b in range(4):
-                c0 = (4 * h + b) * P
-                nc.tensor.transpose(back[:, b, :], spread[:, c0 : c0 + P], ident[:])
-            spread_copy(out=gains[:, 512 * h : 512 * (h + 1)], in_=back[:].rearrange("p b n -> p (b n)"))
+        for h in range(S // BANK_WORDS):
+            back = psum.tile([P, blocks, P], F32, name="back%d" % h, tag="bank%d" % (6 + h))
+            for b in range(blocks):
+                j0 = (blocks * h + b) * P
+                nc.tensor.transpose(back[:, b, :], spread[:, j0 : j0 + P], ident[:])
+            nc.scalar.copy(
+                out=gains[:, BANK_WORDS * h : BANK_WORDS * (h + 1)], in_=back[:].rearrange("p b n -> p (b n)")
+            )
 
         u_codes = keep.tile([P, M], U32, name="u_codes", align_bytes=64)
         u_scales = keep.tile([P, M], U8, name="u_scales", align_bytes=64)
-        banks = [psum.tile([P, GROUP], F32, name="bank%d" % g, tag="bank%d" % g) for g in range(S // GROUP)]
+        banks = [
+            psum.tile([P, BANK_COLUMNS], F32, name="bank%d" % g, tag="bank%d" % g) for g in range(S // BANK_COLUMNS)
+        ]
 
-        def place(s, tag):
-            s0, sw = scatters[s]
-            sums = keep.tile([P, sw], F32, name="sum%d" % s, tag=tag)
-            for g0 in range(s0, s0 + sw, GROUP):
-                part = sums[:, g0 - s0 : g0 - s0 + GROUP]
-                if EMPTY[s] == "m":
-                    nc.vector.tensor_tensor(part, banks[g0 // GROUP][:], gains[:, g0 : g0 + GROUP], mybir.AluOpType.mult)
-                elif EMPTY[s] == "s":
-                    nc.scalar.copy(out=part, in_=banks[g0 // GROUP][:])
-                else:
-                    nc.vector.tensor_copy(out=part, in_=banks[g0 // GROUP][:])
-            places = window[:].indirect(offsets[:, s0 // 16 : (s0 + sw) // 16])
-            if EMPTY[s] == "m":
-                nc.vector.tensor_copy(out=places, in_=sums[:])
-            else:
-                nc.vector.tensor_tensor(places, sums[:], gains[:, s0 : s0 + sw], mybir.AluOpType.mult)
+        def place(first, tag):
+            sums = keep.tile([P, QUARTER], F32, name="sums%d" % first, tag=tag)
+            for j0 in range(0, QUARTER, BANK_COLUMNS):
+                nc.scalar.copy(out=sums[:, j0 : j0 + BANK_COLUMNS], in_=banks[(first + j0) // BANK_COLUMNS][:])
+            nc.vector.tensor_tensor(
+                window[:].indirect(offsets[:, first // LIST_ROWS : (first + QUARTER) // LIST_ROWS]),
+                sums[:],
+                gains[:, first : first + QUARTER],
+                mybir.AluOpType.mult,
+            )
 
-        for i, (a, c0, w) in enumerate(loads):
-            grouped = keep.tile([P, w, PACK], BF16, name="grouped%d" % i, align_bytes=64)
-            codes = keep.tile([P, w], U32, name="codes%d" % i, align_bytes=64)
-            scales = keep.tile([P, w], U8, name="scales%d" % i, align_bytes=64)
-            share = SHARES[i]
-            h0 = 0
-            while h0 < w:
-                hw = max(v for v in (128, 256, 512) if v <= min(PIECE_LAST if a == X_PASSES else PIECE, w - h0))
-                wg = hw * POOL[i] // 16
-                ws = min(hw - wg, hw * share // 16)
-                if ws > 0:
-                    interleave(nc.scalar.copy, grouped, raws[i], h0, h0 + ws)
-                if wg > 0:
-                    interleave(nc.gpsimd.tensor_copy, grouped, raws[i], h0 + ws, h0 + ws + wg)
-                if ws + wg < hw:
-                    interleave(nc.vector.tensor_copy, grouped, raws[i], h0 + ws + wg, h0 + hw)
-                nc.vector.quantize_mx(
-                    out=codes[:, h0 : h0 + hw].bitcast(FP8X4),
-                    scales=scales[:, h0 : h0 + hw],
-                    in_=grouped[:, h0 : h0 + hw, :].rearrange("p w j -> p (w j)"),
-                )
-                h0 += hw
-            if i == U_AT:
+        for i, (a, first, width) in enumerate(loads):
+            grouped = keep.tile([P, width, PACK], BF16, name="grouped%d" % i, align_bytes=64)
+            codes = keep.tile([P, width], U32, name="codes%d" % i, align_bytes=64)
+            scales = keep.tile([P, width], U8, name="scales%d" % i, align_bytes=64)
+            step = min(width, QUANTISE_COLUMNS)
+            on_scalar = step if (a, first) in scalar_alone else step * SCALAR_SIXTEENTHS // 16
+            for lo in range(0, width, step):
+                interleave(nc.scalar.copy, grouped, raws[i], lo, lo + on_scalar)
+                if on_scalar < step:
+                    interleave(nc.vector.tensor_copy, grouped, raws[i], lo + on_scalar, lo + step)
+                quantise(codes[:, lo : lo + step], scales[:, lo : lo + step], grouped[:, lo : lo + step, :])
+
+            if a == 1:
                 u_grouped = keep.tile([P, M, PACK], BF16, name="u_grouped", align_bytes=64)
                 interleave(nc.vector.tensor_copy, u_grouped, u_raw, 0, M)
-                nc.vector.quantize_mx(
-                    out=u_codes[:].bitcast(FP8X4), scales=u_scales[:], in_=u_grouped[:].rearrange("p w j -> p (w j)")
-                )
-            for s in range(len(scatters)):
-                if HOLD[s] == i:
-                    place(s, "raw%d" % i)
-            for g0 in range(c0, c0 + w, GROUP):
-                cols = slice(g0 - c0, g0 - c0 + GROUP)
+                quantise(u_codes[:], u_scales[:], u_grouped[:])
+
+            if a == C_PASS - 1 and first > 0:
+                place(first - QUARTER, "raw%d" % i)
+
+            for j0 in range(0, width, BANK_COLUMNS):
+                cols = slice(j0, j0 + BANK_COLUMNS)
                 nc.tensor.matmul_mx(
-                    out=banks[g0 // GROUP][:],
-                    lhsT=w_words[:, a, :].bitcast(FP4X4) if a < X_PASSES else u_codes[:].bitcast(FP8X4),
-                    lhsT_scale=w_scales[:, a, :] if a < X_PASSES else u_scales[:],
+                    out=banks[(first + j0) // BANK_COLUMNS][:],
+                    lhsT=u_codes[:].bitcast(FP8X4) if a == C_PASS else w_words[:, a, :].bitcast(FP4X4),
+                    lhsT_scale=u_scales[:] if a == C_PASS else w_scales[:, a, :],
                     rhs=codes[:, cols].bitcast(FP8X4),
                     rhs_scale=scales[:, cols],
                     start=(a == 0),
-                    stop=(a == X_PASSES),
+                    stop=(a == C_PASS),
                 )
-            for s, (s0, sw) in enumerate(scatters):
-                if a == X_PASSES and c0 < s0 + sw <= c0 + w and HOLD[s] < 0:
-                    place(s, "sum%d" % s)
 
+        place(S - QUARTER, "last_sums")
         nc.sync.dma_start(out=out, in_=window[:])

@@ -22,6 +22,7 @@ X_PASSES = K // K_PASS
 C_PASS = X_PASSES
 LIST_ROWS = 16
 LISTS = P // LIST_ROWS
+FIRST_GAIN_ROW = P - 2 * LISTS
 BANK_COLUMNS = 128
 BANK_WORDS = 512
 
@@ -58,22 +59,23 @@ def tile_list_hscat_d_none_kernel(tc, x, w4_words, w4_scales, c, u, wgo, offs, o
         w_scales = keep.tile([P, X_PASSES, M], U8, name="w_scales", align_bytes=64)
         u_raw = keep.tile([P, PACK, M], F32, name="u_raw")
         gains = keep.tile([P, S], F32, name="gains")
-        list_gains = keep.tile([P, S], F32, name="list_gains")
+        list_gains = keep.tile([P, S // 2], F32, name="list_gains")
         spread = keep.tile([P, S], F32, name="spread")
         ident = keep.tile([P, P], F32, name="ident")
 
         nc.vector.memset(w_scales[:].rearrange("p a n -> p (a n)").bitcast(I32), 0)
-        nc.gpsimd.memset(list_gains[:], 0.0)
+        nc.gpsimd.memset(list_gains[0:FIRST_GAIN_ROW, :], 0.0)
         nc.vector.memset(window[:], 0.0)
         make_identity(nc, ident[:])
 
+        half_rows = wgo.rearrange("n (h w) -> (n h) w", h=2)
+        nc.scalar.dma_start(out=list_gains[FIRST_GAIN_ROW:P, :], in_=half_rows[0 : 2 * P : LIST_ROWS + 1, :])
         nc.scalar.dma_start(out=w_words[:].bitcast(I32), in_=w4_words.rearrange("a p b -> p a b").bitcast(I32))
         for q in range(4):
             nc.scalar.dma_start(
                 out=w_scales[32 * q : 32 * q + 4, :, :].bitcast(I32),
                 in_=w4_scales[:, 4 * q : 4 * q + 4, :].rearrange("a r n -> r a n").bitcast(I32),
             )
-        nc.scalar.dma_start(out=list_gains[0:P:LIST_ROWS, :], in_=wgo[0:P:LIST_ROWS, :])
 
         raws = []
         for i, (a, first, width) in enumerate(loads):
@@ -87,16 +89,15 @@ def tile_list_hscat_d_none_kernel(tc, x, w4_words, w4_scales, c, u, wgo, offs, o
                 nc.sync.dma_start(offsets[:], offs)
 
         blocks = BANK_WORDS // P
+        turned = psum.tile([P, blocks, P], F32, name="turned", tag="bank4")
+        for b in range(blocks):
+            nc.tensor.transpose(turned[:, b, :], list_gains[:, b * P : (b + 1) * P], ident[:])
         for h in range(S // BANK_WORDS):
-            turned = psum.tile([P, blocks, P], F32, name="turned%d" % h, tag="bank%d" % (4 + h))
-            for b in range(blocks):
-                j0 = (blocks * h + b) * P
-                nc.tensor.transpose(turned[:, b, :], list_gains[:, j0 : j0 + P], ident[:])
             nc.scalar.copy(
                 out=spread[:, BANK_WORDS * h : BANK_WORDS * (h + 1)].rearrange(
                     "p (b g r) -> p b g r", b=blocks, g=LISTS
                 ),
-                in_=turned[:, :, 0:P:LIST_ROWS].unsqueeze(3).to_broadcast([P, blocks, LISTS, LIST_ROWS]),
+                in_=turned[:, :, FIRST_GAIN_ROW + h : P : 2].unsqueeze(3).to_broadcast([P, blocks, LISTS, LIST_ROWS]),
             )
         for h in range(S // BANK_WORDS):
             back = psum.tile([P, blocks, P], F32, name="back%d" % h, tag="bank%d" % (6 + h))

@@ -47,7 +47,6 @@ def tile_list_hscat_d_none_kernel(tc, x, w4_words, w4_scales, c, u, wgo, offs, o
     loads = [(a, 0, S) for a in range(FULL_PASSES)]
     for first in range(0, S, QUARTER):
         loads.extend((a, first, QUARTER) for a in range(FULL_PASSES, C_PASS + 1))
-    scalar_alone = [(C_PASS, QUARTER), (C_PASS - 1, 2 * QUARTER), (C_PASS - 1, 3 * QUARTER)]
 
     with ExitStack() as ctx:
         keep = ctx.enter_context(tc.tile_pool(name="keep", bufs=1))
@@ -80,7 +79,7 @@ def tile_list_hscat_d_none_kernel(tc, x, w4_words, w4_scales, c, u, wgo, offs, o
         raws = []
         for i, (a, first, width) in enumerate(loads):
             rows = c if a == C_PASS else x[a * K_PASS : (a + 1) * K_PASS, :]
-            raw = keep.tile([P, PACK, width], F32, name="raw%d" % i, tag="raw%d" % i)
+            raw = keep.tile([P, PACK, width], F32, name="raw%d" % i, tag="raw%d" % i, align_bytes=64)
             nc.sync.dma_start(out=raw[:], in_=rows[:, first : first + width].rearrange("(p t) w -> p t w", t=PACK))
             raws.append(raw)
             if a == 1:
@@ -115,7 +114,7 @@ def tile_list_hscat_d_none_kernel(tc, x, w4_words, w4_scales, c, u, wgo, offs, o
         ]
 
         def place(first, tag):
-            sums = keep.tile([P, QUARTER], F32, name="sums%d" % first, tag=tag)
+            sums = keep.tile([P, QUARTER], F32, name="sums%d" % first, tag=tag, align_bytes=64)
             for j0 in range(0, QUARTER, BANK_COLUMNS):
                 nc.scalar.copy(out=sums[:, j0 : j0 + BANK_COLUMNS], in_=banks[(first + j0) // BANK_COLUMNS][:])
             nc.vector.tensor_tensor(
@@ -125,30 +124,26 @@ def tile_list_hscat_d_none_kernel(tc, x, w4_words, w4_scales, c, u, wgo, offs, o
                 mybir.AluOpType.mult,
             )
 
-        for i, (a, first, width) in enumerate(loads):
-            grouped = keep.tile([P, width, PACK], BF16, name="grouped%d" % i, align_bytes=64)
-            codes = keep.tile([P, width], U32, name="codes%d" % i, align_bytes=64)
-            scales = keep.tile([P, width], U8, name="scales%d" % i, align_bytes=64)
-            step = min(width, QUANTISE_COLUMNS)
-            on_scalar = step if (a, first) in scalar_alone else step * SCALAR_SIXTEENTHS // 16
-            for lo in range(0, width, step):
-                interleave(nc.scalar.copy, grouped, raws[i], lo, lo + on_scalar)
-                if on_scalar < step:
-                    interleave(nc.vector.tensor_copy, grouped, raws[i], lo + on_scalar, lo + step)
-                quantise(codes[:, lo : lo + step], scales[:, lo : lo + step], grouped[:, lo : lo + step, :])
+        grouped = {}
 
-            if a == 1:
-                u_grouped = keep.tile([P, M, PACK], BF16, name="u_grouped", align_bytes=64)
-                interleave(nc.vector.tensor_copy, u_grouped, u_raw, 0, M)
-                quantise(u_codes[:], u_scales[:], u_grouped[:])
+        def spread_rows(i, lo, hi, sixteenths, tag):
+            if i not in grouped:
+                grouped[i] = keep.tile([P, loads[i][2], PACK], BF16, name="grouped%d" % i, tag=tag, align_bytes=64)
+            cut = lo + (hi - lo) * sixteenths // 16
+            if cut > lo:
+                interleave(nc.scalar.copy, grouped[i], raws[i], lo, cut)
+            if cut < hi:
+                interleave(nc.vector.tensor_copy, grouped[i], raws[i], cut, hi)
 
-            if a == C_PASS - 1 and first > 0:
-                place(first - QUARTER, "raw%d" % i)
-
-            for j0 in range(0, width, BANK_COLUMNS):
+        def multiply(i, lo, hi, tag=None):
+            a, first, width = loads[i]
+            codes = keep.tile([P, hi - lo], U32, name="codes%d_%d" % (i, lo), tag=tag or "codes%d_%d" % (i, lo), align_bytes=64)
+            scales = keep.tile([P, hi - lo], U8, name="scales%d_%d" % (i, lo), align_bytes=64)
+            quantise(codes[:], scales[:], grouped[i][:, lo:hi, :])
+            for j0 in range(0, hi - lo, BANK_COLUMNS):
                 cols = slice(j0, j0 + BANK_COLUMNS)
                 nc.tensor.matmul_mx(
-                    out=banks[(first + j0) // BANK_COLUMNS][:],
+                    out=banks[(first + lo + j0) // BANK_COLUMNS][:],
                     lhsT=u_codes[:].bitcast(FP8X4) if a == C_PASS else w_words[:, a, :].bitcast(FP4X4),
                     lhsT_scale=u_scales[:] if a == C_PASS else w_scales[:, a, :],
                     rhs=codes[:, cols].bitcast(FP8X4),
@@ -157,5 +152,38 @@ def tile_list_hscat_d_none_kernel(tc, x, w4_words, w4_scales, c, u, wgo, offs, o
                     stop=(a == C_PASS),
                 )
 
+        half = QUANTISE_COLUMNS
+        for i in range(FULL_PASSES):
+            spread_rows(i, 0, half, SCALAR_SIXTEENTHS, "grouped%d" % i)
+            spread_rows(i, half, S, SCALAR_SIXTEENTHS, "grouped%d" % i)
+            multiply(i, 0, half)
+            if i < FULL_PASSES - 1:
+                multiply(i, half, S)
+            if i == 1:
+                u_grouped = keep.tile([P, M, PACK], BF16, name="u_grouped", align_bytes=64)
+                interleave(nc.vector.tensor_copy, u_grouped, u_raw, 0, M)
+                quantise(u_codes[:], u_scales[:], u_grouped[:])
+
+        x0, c0, x1, c1, x2, c2, x3, c3 = range(FULL_PASSES, len(loads))
+        spread_rows(x0, 0, QUARTER, SCALAR_SIXTEENTHS, "grouped_x0")
+        multiply(FULL_PASSES - 1, half, S)
+        spread_rows(c0, 0, QUARTER, SCALAR_SIXTEENTHS, "grouped_c0")
+        multiply(x0, 0, QUARTER)
+        multiply(c0, 0, QUARTER)
+        spread_rows(x1, 0, QUARTER, SCALAR_SIXTEENTHS, "grouped_x1")
+        multiply(x1, 0, QUARTER)
+        place(0, "raw%d" % x1)
+        spread_rows(c1, 0, QUARTER, 16, "grouped_c1")
+        multiply(c1, 0, QUARTER)
+        spread_rows(x2, 0, QUARTER, 16, "grouped_x2")
+        multiply(x2, 0, QUARTER)
+        place(QUARTER, "raw%d" % x2)
+        spread_rows(c2, 0, QUARTER, SCALAR_SIXTEENTHS, "grouped_c2")
+        multiply(c2, 0, QUARTER)
+        spread_rows(x3, 0, QUARTER, 16, "grouped_x3")
+        multiply(x3, 0, QUARTER)
+        place(2 * QUARTER, "raw%d" % x3)
+        spread_rows(c3, 0, QUARTER, SCALAR_SIXTEENTHS, "grouped_c3")
+        multiply(c3, 0, QUARTER)
         place(S - QUARTER, "last_sums")
         nc.sync.dma_start(out=out, in_=window[:])

@@ -176,14 +176,14 @@ def tile_list_hscat_d_none_kernel(tc, x, w4_words, w4_scales, c, u, wgo, offs, o
         spread_rows(c1, 0, QUARTER, 16, "grouped_c1")
         multiply(c1, 0, QUARTER)
         spread_rows(x2, 0, QUARTER, 16, "grouped_x2")
+        spread_rows(c2, 0, QUARTER, 6, "grouped_c2")
         multiply(x2, 0, QUARTER)
-        place(QUARTER, "raw%d" % x2)
-        spread_rows(c2, 0, QUARTER, SCALAR_SIXTEENTHS, "grouped_c2")
         multiply(c2, 0, QUARTER)
+        place(QUARTER, "raw%d" % x2)
         spread_rows(x3, 0, QUARTER, 16, "grouped_x3")
+        spread_rows(c3, 0, QUARTER, 6, "grouped_c3")
         multiply(x3, 0, QUARTER)
-        place(2 * QUARTER, "raw%d" % x3)
-        spread_rows(c3, 0, QUARTER, SCALAR_SIXTEENTHS, "grouped_c3")
         multiply(c3, 0, QUARTER)
+        place(2 * QUARTER, "raw%d" % x3)
         place(S - QUARTER, "last_sums")
         nc.sync.dma_start(out=out, in_=window[:])

@@ -53,10 +53,10 @@ def tile_list_hscat_d_none_kernel(tc, x, w4_words, w4_scales, c, u, wgo, offs, o
         psum = ctx.enter_context(tc.psum_pool(name="psum", bufs=1))
 
         offsets = keep.tile([P, S // LIST_ROWS], U16, name="offsets")
-        window = keep.tile([P, T], F32, name="window")
-        w_words = keep.tile([P, X_PASSES, 2 * M], U8, name="w_words", align_bytes=64)
+        window = keep.tile([P, T], F32, name="window", align_bytes=256)
+        w_words = keep.tile([P, X_PASSES, 2 * M], U8, name="w_words", align_bytes=256)
         w_scales = keep.tile([P, X_PASSES, M], U8, name="w_scales", align_bytes=64)
-        u_raw = keep.tile([P, PACK, M], F32, name="u_raw")
+        u_raw = keep.tile([P, PACK, M], F32, name="u_raw", align_bytes=256)
         gains = keep.tile([P, S], F32, name="gains")
         list_gains = keep.tile([P, S // 2], F32, name="list_gains")
         spread = keep.tile([P, S], F32, name="spread")
@@ -79,7 +79,7 @@ def tile_list_hscat_d_none_kernel(tc, x, w4_words, w4_scales, c, u, wgo, offs, o
         raws = []
         for i, (a, first, width) in enumerate(loads):
             rows = c if a == C_PASS else x[a * K_PASS : (a + 1) * K_PASS, :]
-            raw = keep.tile([P, PACK, width], F32, name="raw%d" % i, tag="raw%d" % i, align_bytes=64)
+            raw = keep.tile([P, PACK, width], F32, name="raw%d" % i, tag="raw%d" % i, align_bytes=256)
             nc.sync.dma_start(out=raw[:], in_=rows[:, first : first + width].rearrange("(p t) w -> p t w", t=PACK))
             raws.append(raw)
             if a == 1:
@@ -114,7 +114,7 @@ def tile_list_hscat_d_none_kernel(tc, x, w4_words, w4_scales, c, u, wgo, offs, o
         ]
 
         def place(first, tag):
-            sums = keep.tile([P, QUARTER], F32, name="sums%d" % first, tag=tag, align_bytes=64)
+            sums = keep.tile([P, QUARTER], F32, name="sums%d" % first, tag=tag, align_bytes=256)
             for j0 in range(0, QUARTER, BANK_COLUMNS):
                 nc.scalar.copy(out=sums[:, j0 : j0 + BANK_COLUMNS], in_=banks[(first + j0) // BANK_COLUMNS][:])
             nc.vector.tensor_tensor(

@@ -79,8 +79,9 @@ def tile_list_hscat_d_none_kernel(tc, x, w4_words, w4_scales, c, u, wgo, offs, o
         raws = []
         for i, (a, first, width) in enumerate(loads):
             rows = c if a == C_PASS else x[a * K_PASS : (a + 1) * K_PASS, :]
-            raw = keep.tile([P, PACK, width], F32, name="raw%d" % i, tag="raw%d" % i, align_bytes=256)
-            nc.sync.dma_start(out=raw[:], in_=rows[:, first : first + width].rearrange("(p t) w -> p t w", t=PACK))
+            pitch = width if width == S else width + 64
+            raw = keep.tile([P, PACK, pitch], F32, name="raw%d" % i, tag="raw%d" % i, align_bytes=256)[:, :, 0:width]
+            nc.sync.dma_start(out=raw, in_=rows[:, first : first + width].rearrange("(p t) w -> p t w", t=PACK))
             raws.append(raw)
             if a == 1:
                 nc.sync.dma_start(out=u_raw[:], in_=u.rearrange("(p t) n -> p t n", t=PACK))

@@ -29,7 +29,7 @@ BANK_WORDS = 512
 FULL_PASSES = 3
 QUARTER = S // 4
 QUANTISE_COLUMNS = 512
-SCALAR_SIXTEENTHS = 6
+SCALAR_SIXTEENTHS = 7
 
 
 def tile_list_hscat_d_none_kernel(tc, x, w4_words, w4_scales, c, u, wgo, offs, out):

@@ -23,13 +23,15 @@ C_PASS = X_PASSES
 LIST_ROWS = 16
 LISTS = P // LIST_ROWS
 FIRST_GAIN_ROW = P - 2 * LISTS
-BANK_COLUMNS = 128
+BANK_COLUMNS = 256
 BANK_WORDS = 512
 
 FULL_PASSES = 3
 QUARTER = S // 4
 QUANTISE_COLUMNS = 512
 SCALAR_SIXTEENTHS = 7
+LEAD = 64
+SPARE = QUARTER - LEAD
 
 
 def tile_list_hscat_d_none_kernel(tc, x, w4_words, w4_scales, c, u, wgo, offs, out):
@@ -77,10 +79,13 @@ def tile_list_hscat_d_none_kernel(tc, x, w4_words, w4_scales, c, u, wgo, offs, o
             )
 
         raws = []
+        wholes = []
         for i, (a, first, width) in enumerate(loads):
             rows = c if a == C_PASS else x[a * K_PASS : (a + 1) * K_PASS, :]
-            pitch = width if width == S else width + 64
-            raw = keep.tile([P, PACK, pitch], F32, name="raw%d" % i, tag="raw%d" % i, align_bytes=256)[:, :, 0:width]
+            pitch = width if width == S else width + (SPARE if i >= len(loads) - 3 and a == C_PASS else 64)
+            whole = keep.tile([P, PACK, pitch], F32, name="raw%d" % i, tag="raw%d" % i, align_bytes=256)
+            wholes.append(whole)
+            raw = whole[:, :, 0:width]
             nc.sync.dma_start(out=raw, in_=rows[:, first : first + width].rearrange("(p t) w -> p t w", t=PACK))
             raws.append(raw)
             if a == 1:
@@ -114,13 +119,16 @@ def tile_list_hscat_d_none_kernel(tc, x, w4_words, w4_scales, c, u, wgo, offs, o
             psum.tile([P, BANK_COLUMNS], F32, name="bank%d" % g, tag="bank%d" % g) for g in range(S // BANK_COLUMNS)
         ]
 
-        def place(first, tag):
-            sums = keep.tile([P, QUARTER], F32, name="sums%d" % first, tag=tag, align_bytes=256)
+        def place(first, tag, over=None):
+            if over is None:
+                sums = keep.tile([P, QUARTER], F32, name="sums%d" % first, tag=tag, align_bytes=256)[:]
+            else:
+                sums = wholes[over][:].rearrange("p t w -> p (t w)")[:, QUARTER : 2 * QUARTER]
             for j0 in range(0, QUARTER, BANK_COLUMNS):
                 nc.scalar.copy(out=sums[:, j0 : j0 + BANK_COLUMNS], in_=banks[(first + j0) // BANK_COLUMNS][:])
             nc.vector.tensor_tensor(
                 window[:].indirect(offsets[:, first // LIST_ROWS : (first + QUARTER) // LIST_ROWS]),
-                sums[:],
+                sums,
                 gains[:, first : first + QUARTER],
                 mybir.AluOpType.mult,
             )
@@ -176,15 +184,14 @@ def tile_list_hscat_d_none_kernel(tc, x, w4_words, w4_scales, c, u, wgo, offs, o
         place(0, "raw%d" % x1)
         spread_rows(c1, 0, QUARTER, 16, "grouped_c1")
         multiply(c1, 0, QUARTER)
-        spread_rows(x2, 0, QUARTER, 16, "grouped_x2")
-        spread_rows(c2, 0, QUARTER, 6, "grouped_c2")
-        multiply(x2, 0, QUARTER)
-        multiply(c2, 0, QUARTER)
-        place(QUARTER, "raw%d" % x2)
-        spread_rows(x3, 0, QUARTER, 16, "grouped_x3")
-        spread_rows(c3, 0, QUARTER, 6, "grouped_c3")
-        multiply(x3, 0, QUARTER)
-        multiply(c3, 0, QUARTER)
-        place(2 * QUARTER, "raw%d" % x3)
+        for x_load, c_load, cut in ((x2, c2, 96), (x3, c3, 128)):
+            spread_rows(x_load, 0, QUARTER, 16, "grouped%d" % x_load)
+            spread_rows(c_load, 0, LEAD, 16, "grouped%d" % c_load)
+            spread_rows(c_load, LEAD, cut, 16, "grouped%d" % c_load)
+            spread_rows(c_load, cut, QUARTER, 0, "grouped%d" % c_load)
+            multiply(x_load, 0, QUARTER)
+            multiply(c_load, 0, QUARTER)
+            place(loads[c_load][1] - QUARTER, None, c_load)
         place(S - QUARTER, "last_sums")
+
         nc.sync.dma_start(out=out, in_=window[:])

@@ -32,6 +32,7 @@ QUANTISE_COLUMNS = 512
 SCALAR_SIXTEENTHS = 7
 LEAD = 64
 SPARE = QUARTER - LEAD
+HOLDERS = (5, 8, 10)
 
 
 def tile_list_hscat_d_none_kernel(tc, x, w4_words, w4_scales, c, u, wgo, offs, out):
@@ -82,7 +83,7 @@ def tile_list_hscat_d_none_kernel(tc, x, w4_words, w4_scales, c, u, wgo, offs, o
         wholes = []
         for i, (a, first, width) in enumerate(loads):
             rows = c if a == C_PASS else x[a * K_PASS : (a + 1) * K_PASS, :]
-            pitch = width if width == S else width + (SPARE if i >= len(loads) - 3 and a == C_PASS else 64)
+            pitch = width if width == S else width + (SPARE if i in HOLDERS else 64)
             whole = keep.tile([P, PACK, pitch], F32, name="raw%d" % i, tag="raw%d" % i, align_bytes=256)
             wholes.append(whole)
             raw = whole[:, :, 0:width]
@@ -90,7 +91,7 @@ def tile_list_hscat_d_none_kernel(tc, x, w4_words, w4_scales, c, u, wgo, offs, o
             raws.append(raw)
             if a == 1:
                 nc.sync.dma_start(out=u_raw[:], in_=u.rearrange("(p t) n -> p t n", t=PACK))
-            if a == C_PASS and first == 0:
+            if a == FULL_PASSES and first == QUARTER:
                 nc.sync.dma_start(offsets[:], offs)
 
         blocks = BANK_WORDS // P
@@ -179,9 +180,11 @@ def tile_list_hscat_d_none_kernel(tc, x, w4_words, w4_scales, c, u, wgo, offs, o
         spread_rows(c0, 0, QUARTER, SCALAR_SIXTEENTHS, "grouped_c0")
         multiply(x0, 0, QUARTER)
         multiply(c0, 0, QUARTER)
-        spread_rows(x1, 0, QUARTER, SCALAR_SIXTEENTHS, "grouped_x1")
+        spread_rows(x1, 0, LEAD, 16, "grouped_x1")
+        spread_rows(x1, LEAD, 96, 16, "grouped_x1")
+        spread_rows(x1, 96, QUARTER, 0, "grouped_x1")
         multiply(x1, 0, QUARTER)
-        place(0, "raw%d" % x1)
+        place(0, None, x1)
         spread_rows(c1, 0, QUARTER, 16, "grouped_c1")
         multiply(c1, 0, QUARTER)
         for x_load, c_load, cut in ((x2, c2, 96), (x3, c3, 128)):

from contextlib import ExitStack

import concourse.mybir as mybir
from concourse.masks import make_identity

K, M, T, S, L = 2048, 128, 2048, 1024, 512
FLOPS = 2 * (K + L) * M * S

F32 = mybir.dt.float32
BF16 = mybir.dt.bfloat16
I32 = mybir.dt.int32
U32 = mybir.dt.uint32
U16 = mybir.dt.uint16
U8 = mybir.dt.uint8
FP8X4 = mybir.dt.float8_e4m3fn_x4
FP4X4 = mybir.dt.float4_e2m1fn_x4

P = 128
PACK = 4
K_PASS = P * PACK
X_PASSES = K // K_PASS
C_PASS = X_PASSES
LIST_ROWS = 16
LISTS = P // LIST_ROWS
FIRST_GAIN_ROW = P - 2 * LISTS
BANK_COLUMNS = 256
BANK_WORDS = 512

FULL_PASSES = 3
QUARTER = S // 4
QUANTISE_COLUMNS = 512
SCALAR_SIXTEENTHS = 7
LEAD = 64
SPARE = QUARTER - LEAD
HOLDERS = (5, 8, 10)


def tile_list_hscat_d_none_kernel(tc, x, w4_words, w4_scales, c, u, wgo, offs, out):
    nc = tc.nc

    def interleave(engine_copy, dst, src, lo, hi):
        engine_copy(
            out=dst[:, lo:hi, :].rearrange("p (c i) t -> p c t i", i=4),
            in_=src[:, :, lo:hi].rearrange("p t (c i) -> p c t i", i=4),
        )

    def quantise(codes, scales, grouped):
        nc.vector.quantize_mx(out=codes.bitcast(FP8X4), scales=scales, in_=grouped.rearrange("p w t -> p (w t)"))

    loads = [(a, 0, S) for a in range(FULL_PASSES)]
    for first in range(0, S, QUARTER):
        loads.extend((a, first, QUARTER) for a in range(FULL_PASSES, C_PASS + 1))

    with ExitStack() as ctx:
        keep = ctx.enter_context(tc.tile_pool(name="keep", bufs=1))
        psum = ctx.enter_context(tc.psum_pool(name="psum", bufs=1))

        offsets = keep.tile([P, S // LIST_ROWS], U16, name="offsets")
        window = keep.tile([P, T], F32, name="window", align_bytes=256)
        w_words = keep.tile([P, X_PASSES, 2 * M], U8, name="w_words", align_bytes=256)
        w_scales = keep.tile([P, X_PASSES, M], U8, name="w_scales", align_bytes=64)
        u_raw = keep.tile([P, PACK, M], F32, name="u_raw", align_bytes=256)
        gains = keep.tile([P, S], F32, name="gains")
        list_gains = keep.tile([P, S // 2], F32, name="list_gains")
        spread = keep.tile([P, S], F32, name="spread")
        ident = keep.tile([P, P], F32, name="ident")

        nc.vector.memset(w_scales[:].rearrange("p a n -> p (a n)").bitcast(I32), 0)
        nc.gpsimd.memset(list_gains[0:FIRST_GAIN_ROW, :], 0.0)
        nc.vector.memset(window[:], 0.0)
        make_identity(nc, ident[:])

        half_rows = wgo.rearrange("n (h w) -> (n h) w", h=2)
        nc.scalar.dma_start(out=list_gains[FIRST_GAIN_ROW:P, :], in_=half_rows[0 : 2 * P : LIST_ROWS + 1, :])
        nc.scalar.dma_start(out=w_words[:].bitcast(I32), in_=w4_words.rearrange("a p b -> p a b").bitcast(I32))
        for q in range(4):
            nc.scalar.dma_start(
                out=w_scales[32 * q : 32 * q + 4, :, :].bitcast(I32),
                in_=w4_scales[:, 4 * q : 4 * q + 4, :].rearrange("a r n -> r a n").bitcast(I32),
            )

        raws = []
        wholes = []
        for i, (a, first, width) in enumerate(loads):
            rows = c if a == C_PASS else x[a * K_PASS : (a + 1) * K_PASS, :]
            pitch = width if width == S else width + (SPARE if i in HOLDERS else 64)
            whole = keep.tile([P, PACK, pitch], F32, name="raw%d" % i, tag="raw%d" % i, align_bytes=256)
            wholes.append(whole)
            raw = whole[:, :, 0:width]
            nc.sync.dma_start(out=raw, in_=rows[:, first : first + width].rearrange("(p t) w -> p t w", t=PACK))
            raws.append(raw)
            if a == 1:
                nc.sync.dma_start(out=u_raw[:], in_=u.rearrange("(p t) n -> p t n", t=PACK))
            if a == FULL_PASSES and first == QUARTER:
                nc.sync.dma_start(offsets[:], offs)

        blocks = BANK_WORDS // P
        turned = psum.tile([P, blocks, P], F32, name="turned", tag="bank4")
        for b in range(blocks):
            nc.tensor.transpose(turned[:, b, :], list_gains[:, b * P : (b + 1) * P], ident[:])
        for h in range(S // BANK_WORDS):
            nc.scalar.copy(
                out=spread[:, BANK_WORDS * h : BANK_WORDS * (h + 1)].rearrange(
                    "p (b g r) -> p b g r", b=blocks, g=LISTS
                ),
                in_=turned[:, :, FIRST_GAIN_ROW + h : P : 2].unsqueeze(3).to_broadcast([P, blocks, LISTS, LIST_ROWS]),
            )
        for h in range(S // BANK_WORDS):
            back = psum.tile([P, blocks, P], F32, name="back%d" % h, tag="bank%d" % (6 + h))
            for b in range(blocks):
                j0 = (blocks * h + b) * P
                nc.tensor.transpose(back[:, b, :], spread[:, j0 : j0 + P], ident[:])
            nc.scalar.copy(
                out=gains[:, BANK_WORDS * h : BANK_WORDS * (h + 1)], in_=back[:].rearrange("p b n -> p (b n)")
            )

        u_codes = keep.tile([P, M], U32, name="u_codes", align_bytes=64)
        u_scales = keep.tile([P, M], U8, name="u_scales", align_bytes=64)
        banks = [
            psum.tile([P, BANK_COLUMNS], F32, name="bank%d" % g, tag="bank%d" % g) for g in range(S // BANK_COLUMNS)
        ]

        def place(first, tag, over=None):
            if over is None:
                sums = keep.tile([P, QUARTER], F32, name="sums%d" % first, tag=tag, align_bytes=256)[:]
            else:
                sums = wholes[over][:].rearrange("p t w -> p (t w)")[:, QUARTER : 2 * QUARTER]
            for j0 in range(0, QUARTER, BANK_COLUMNS):
                nc.scalar.copy(out=sums[:, j0 : j0 + BANK_COLUMNS], in_=banks[(first + j0) // BANK_COLUMNS][:])
            nc.vector.tensor_tensor(
                window[:].indirect(offsets[:, first // LIST_ROWS : (first + QUARTER) // LIST_ROWS]),
                sums,
                gains[:, first : first + QUARTER],
                mybir.AluOpType.mult,
            )

        grouped = {}

        def spread_rows(i, lo, hi, sixteenths, tag):
            if i not in grouped:
                grouped[i] = keep.tile([P, loads[i][2], PACK], BF16, name="grouped%d" % i, tag=tag, align_bytes=64)
            cut = lo + (hi - lo) * sixteenths // 16
            if cut > lo:
                interleave(nc.scalar.copy, grouped[i], raws[i], lo, cut)
            if cut < hi:
                interleave(nc.vector.tensor_copy, grouped[i], raws[i], cut, hi)

        def multiply(i, lo, hi, tag=None):
            a, first, width = loads[i]
            codes = keep.tile([P, hi - lo], U32, name="codes%d_%d" % (i, lo), tag=tag or "codes%d_%d" % (i, lo), align_bytes=64)
            scales = keep.tile([P, hi - lo], U8, name="scales%d_%d" % (i, lo), align_bytes=64)
            quantise(codes[:], scales[:], grouped[i][:, lo:hi, :])
            for j0 in range(0, hi - lo, BANK_COLUMNS):
                cols = slice(j0, j0 + BANK_COLUMNS)
                nc.tensor.matmul_mx(
                    out=banks[(first + lo + j0) // BANK_COLUMNS][:],
                    lhsT=u_codes[:].bitcast(FP8X4) if a == C_PASS else w_words[:, a, :].bitcast(FP4X4),
                    lhsT_scale=u_scales[:] if a == C_PASS else w_scales[:, a, :],
                    rhs=codes[:, cols].bitcast(FP8X4),
                    rhs_scale=scales[:, cols],
                    start=(a == 0),
                    stop=(a == C_PASS),
                )

        half = QUANTISE_COLUMNS
        for i in range(FULL_PASSES):
            spread_rows(i, 0, half, SCALAR_SIXTEENTHS, "grouped%d" % i)
            spread_rows(i, half, S, SCALAR_SIXTEENTHS, "grouped%d" % i)
            multiply(i, 0, half)
            if i < FULL_PASSES - 1:
                multiply(i, half, S)
            if i == 1:
                u_grouped = keep.tile([P, M, PACK], BF16, name="u_grouped", align_bytes=64)
                interleave(nc.vector.tensor_copy, u_grouped, u_raw, 0, M)
                quantise(u_codes[:], u_scales[:], u_grouped[:])

        x0, c0, x1, c1, x2, c2, x3, c3 = range(FULL_PASSES, len(loads))
        spread_rows(x0, 0, QUARTER, SCALAR_SIXTEENTHS, "grouped_x0")
        multiply(FULL_PASSES - 1, half, S)
        spread_rows(c0, 0, QUARTER, SCALAR_SIXTEENTHS, "grouped_c0")
        multiply(x0, 0, QUARTER)
        multiply(c0, 0, QUARTER)
        spread_rows(x1, 0, LEAD, 16, "grouped_x1")
        spread_rows(x1, LEAD, 96, 16, "grouped_x1")
        spread_rows(x1, 96, QUARTER, 0, "grouped_x1")
        multiply(x1, 0, QUARTER)
        place(0, None, x1)
        spread_rows(c1, 0, QUARTER, 16, "grouped_c1")
        multiply(c1, 0, QUARTER)
        for x_load, c_load, cut in ((x2, c2, 96), (x3, c3, 128)):
            spread_rows(x_load, 0, QUARTER, 16, "grouped%d" % x_load)
            spread_rows(c_load, 0, LEAD, 16, "grouped%d" % c_load)
            spread_rows(c_load, LEAD, cut, 16, "grouped%d" % c_load)
            spread_rows(c_load, cut, QUARTER, 0, "grouped%d" % c_load)
            multiply(x_load, 0, QUARTER)
            multiply(c_load, 0, QUARTER)
            place(loads[c_load][1] - QUARTER, None, c_load)
        place(S - QUARTER, "last_sums")

        nc.sync.dma_start(out=out, in_=window[:])
